import numpy as np
import ml_dtypes


def mxq(x, axis, fmt="e4m3"):
    dtype, down = {"e4m3": (ml_dtypes.float8_e4m3fn, 7), "e5m2": (ml_dtypes.float8_e5m2, 14)}[fmt]
    v = np.moveaxis(np.asarray(x, np.float32).astype(ml_dtypes.bfloat16).astype(np.float64), axis, -1)
    blocks = v.reshape(v.shape[:-1] + (-1, 32))
    amax = np.abs(blocks).max(-1, keepdims=True)
    byte = np.maximum(np.where(amax > 0, np.frexp(amax)[1] - 1 + 127, 0) - down, 1)
    scale = np.exp2(byte - 127.0)
    codes = (blocks / scale).astype(np.float32).astype(dtype).astype(np.float64)
    return np.moveaxis((codes * scale).reshape(v.shape), -1, axis)


WIDE = False


def mx_kscale(k):
    if not WIDE:
        return np.ones(k)
    levels = np.array([10, -10, 5, -5, 0])
    if k % 512:
        return np.exp2(np.random.permutation(np.resize(levels, k // 32))).repeat(32)
    a = np.empty((k // 512, 16))
    for p in range(k // 512):
        a[p, :8] = np.random.permutation(np.resize(levels, 8))
        for g in range(8):
            far = levels[np.abs(levels - a[p, g]) >= 10]
            a[p, g + 8] = far[np.random.randint(len(far))]
    return np.exp2(a.ravel()).repeat(32)


def f64(x):
    return np.asarray(x).astype(np.float64)


def striped(idx):
    return np.tile(idx.reshape(-1, 16).T, (8, 1)).astype(np.uint16)


def unstriped(offs):
    return offs[:16].T.reshape(-1).astype(np.int64)


def pack_weight(w):
    k, n = w.shape
    w = f64(np.asarray(w, np.float32).astype(ml_dtypes.bfloat16)).reshape(k // 32, 32, n)
    amax = np.abs(w).max(1)
    byte = np.clip(np.where(amax > 0, np.frexp(amax)[1] - 1 + 127 - 7, 1), 1, 254)
    scaled = (w * np.exp2(127.0 - byte)[:, None, :]).reshape(k, n).astype(np.float32)
    words = np.ascontiguousarray(scaled.reshape(k // 512, 128, 4, n).transpose(0, 1, 3, 2)).astype(ml_dtypes.float8_e4m3fn).view(np.uint8)
    return words, np.ascontiguousarray(byte.astype(np.uint8).reshape(k // 512, 16, n))


def unpack_weight(words, scales):
    g, p, n, _ = words.shape
    vals = np.ascontiguousarray(words).view(ml_dtypes.float8_e4m3fn).astype(np.float64) * np.repeat(np.exp2(scales.astype(np.float64) - 127.0), 8, axis=1)[..., None]
    return vals.transpose(0, 1, 3, 2).reshape(g * 512, n)


def planes(y):
    n, m = y.shape
    v = y.astype(np.float32).astype(ml_dtypes.bfloat16).astype(np.float64).reshape(n // 32, 32, m)
    top = np.abs(v).max(1)
    byte = np.clip(np.where(top > 0, np.frexp(top)[1] - 1 + 127 - 7, 1), 1, 254)
    codes = (v * np.exp2(127.0 - byte)[:, None, :]).reshape(n, m).astype(np.float32).astype(ml_dtypes.float8_e4m3fn).view(np.uint8)
    words = codes.reshape(n // 512, 128, 4, m).transpose(0, 1, 3, 2)
    return np.ascontiguousarray(words), np.ascontiguousarray(byte.astype(np.uint8).reshape(n // 512, 16, m))


def sigmoid(v):
    return 1.0 / (1.0 + np.exp(-np.maximum(v, -700.0)))


K, T, S, W, H = 512, 2048, 512, 1024, 512


def setup_inputs():
    n = np.random.standard_normal
    s = mx_kscale(K)[:, None]
    u = mx_kscale(H)
    packed_xT = pack_weight(n((K, T)) * s)
    packed_eT = pack_weight(n((K, W)) * s)
    return {
        "x_words": packed_xT[0],
        "x_scales": packed_xT[1],
        "e_words": packed_eT[0],
        "e_scales": packed_eT[1],
        "w1": (n((K, H)) / np.sqrt(2 * K) / s * u).astype(np.float32),
        "w2": (n((K, H)) / np.sqrt(2 * K) / s * u).astype(np.float32),
        "w3": (n((H, H)) / np.sqrt(H) / u[:, None]).astype(np.float32),
        "skip": (n((H, S)) * u[:, None]).astype(np.float32),
        "offs": striped(np.random.permutation(T)[:S]),
        "tok": striped(np.random.permutation(W)[:S]),
    }


def reference(x_words, x_scales, e_words, e_scales, w1, w2, w3, skip, offs, tok):
    xq = unpack_weight(x_words, x_scales)[:, unstriped(offs)]
    e_tok = unpack_weight(e_words, e_scales)[:, unstriped(tok)]
    h = mxq(f64(w1), 0, "e4m3").T @ xq + mxq(f64(w2), 0, "e4m3").T @ e_tok
    g = sigmoid(mxq(f64(w3), 0, "e4m3").T @ mxq(h, 0, "e4m3"))
    out_0 = f64(skip) + g * (h - f64(skip))
    return (out_0,) + planes(out_0)

@@ -1,0 +1,182 @@
+from contextlib import ExitStack
+
+import concourse.mybir as mybir
+
+F32 = mybir.dt.float32
+BF16 = mybir.dt.bfloat16
+I32 = mybir.dt.int32
+U32 = mybir.dt.uint32
+U16 = mybir.dt.uint16
+U8 = mybir.dt.uint8
+FP8X4 = mybir.dt.float8_e4m3fn_x4
+ALU = mybir.AluOpType
+ACT = mybir.ActivationFunctionType
+
+P = 128
+PACK = 4
+H = 512
+S = 512
+CHUNK = 128
+CHUNKS = S // CHUNK
+QUADS = 4
+FLOPS = 3 * 2 * 512 * 512 * 512
+
+
+def tile_picked_zhwy_lin_po_kernel(
+    tc, x_words, x_scales, e_words, e_scales, w1, w2, w3, skip, offs, tok, out_0, out_1, out_2
+):
+    nc = tc.nc
+    with ExitStack() as ctx:
+        keep = ctx.enter_context(tc.tile_pool(name="keep", bufs=1))
+        psum = ctx.enter_context(tc.psum_pool(name="psum", bufs=1))
+
+        offs_t = keep.tile([P, S // 16], U16, name="offs_t")
+        tok_t = keep.tile([P, S // 16], U16, name="tok_t")
+
+        def clear_plane(name, scales):
+            plane = keep.tile([P, scales.shape[2]], U8, name=name, align_bytes=64)
+            nc.vector.memset(plane[:].bitcast(I32), 0)
+            return plane
+
+        def load_scales(plane, scales):
+            rows = scales[0].bitcast(I32)
+            for q in range(QUADS):
+                nc.sync.dma_start(plane[32 * q : 32 * q + 4, :].bitcast(I32), rows[4 * q : 4 * q + 4, :])
+
+        def load_words(name, words):
+            table = keep.tile([P, words.shape[2]], U32, name=name, align_bytes=64)
+            nc.sync.dma_start(table[:].bitcast(I32), words[0].rearrange("p n t -> p (n t)").bitcast(I32))
+            return table
+
+        def load_rows(name, matrix, c0, c1):
+            piece = keep.tile([P, PACK, c1 - c0], F32, name=name)
+            nc.sync.dma_start(piece[:], matrix.rearrange("(p j) c -> p j c", j=PACK)[:, :, c0:c1])
+            return piece
+
+        x_plane = clear_plane("x_plane", x_scales)
+        e_plane = clear_plane("e_plane", e_scales)
+        warm = keep.tile([P, 2], F32, name="warm")
+        nc.vector.memset(warm[:, 0:1], 0.0)
+        nc.scalar.activation(warm[:, 1:2], warm[:, 0:1], ACT.Sigmoid)
+        w1_lo = load_rows("w1_lo", w1, 0, 256)
+        load_scales(x_plane, x_scales)
+        nc.sync.dma_start(offs_t[:], offs)
+        w1_hi = load_rows("w1_hi", w1, 256, 512)
+        w2_raw = [load_rows("w2_raw", w2, 0, 512)]
+        load_scales(e_plane, e_scales)
+        nc.sync.dma_start(tok_t[:], tok)
+        x_table = load_words("x_table", x_words)
+        e_table = load_words("e_table", e_words)
+        w3_raw = [load_rows("w3_raw%d" % a, w3, 256 * a, 256 * (a + 1)) for a in range(2)]
+        skip_t = [load_rows("skip_t%d" % a, skip, 256 * a, 256 * (a + 1)) for a in range(2)]
+
+        def round_and_deal(engine_copy, dealt, raw, c0, c1, m0):
+            count = (c1 - c0) // PACK
+            engine_copy(
+                dealt[:, :, m0 : m0 + count, :].rearrange("p t m j -> p m t j"),
+                raw[:, :, c0:c1].rearrange("p j (m t) -> p m t j", t=PACK),
+            )
+
+        def quantize_weight(name, dealt):
+            codes = keep.tile([P, H], U32, name=name + "_codes", align_bytes=64)
+            plane = keep.tile([P, H], U8, name=name + "_plane", align_bytes=64)
+            nc.vector.quantize_mx(
+                out=codes[:].bitcast(FP8X4), scales=plane[:], in_=dealt[:].rearrange("p t m j -> p (t m j)")
+            )
+            return codes, plane
+
+        def gather(name, dtype, table, offsets, first, count):
+            picked = keep.tile([P, count], dtype, name=name, align_bytes=64)
+            nc.vector.tensor_copy(picked[:], table[:].indirect(offsets[:, first // 16 : (first + count) // 16]))
+            return picked
+
+        x_bytes = gather("x_bytes", U8, x_plane, offs_t, 0, S)
+        w1_dealt = keep.tile([P, PACK, P, PACK], BF16, name="w1_dealt", align_bytes=64)
+        round_and_deal(nc.scalar.copy, w1_dealt, w1_lo, 0, 256, 0)
+        round_and_deal(nc.vector.tensor_copy, w1_dealt, w1_hi, 0, 256, 64)
+        e_bytes = gather("e_bytes", U8, e_plane, tok_t, 0, S)
+        w1_q = quantize_weight("w1", w1_dealt)
+        w2_dealt = keep.tile([P, PACK, P, PACK], BF16, name="w2_dealt", align_bytes=64)
+        round_and_deal(nc.scalar.copy, w2_dealt, w2_raw[0], 0, 256, 0)
+        round_and_deal(nc.vector.tensor_copy, w2_dealt, w2_raw[0], 256, 512, 64)
+        w2_q = quantize_weight("w2", w2_dealt)
+        x_picked = [gather("x_picked%d" % a, U32, x_table, offs_t, 256 * a, 256) for a in range(2)]
+        e_picked = [gather("e_picked%d" % c, U32, e_table, tok_t, CHUNK * c, CHUNK) for c in range(CHUNKS)]
+
+        def mx(out, weight, t, codes, plane, start, stop):
+            cols = slice(P * t, P * (t + 1))
+            nc.tensor.matmul_mx(
+                out=out,
+                lhsT=weight[0][:, cols].bitcast(FP8X4),
+                lhsT_scale=weight[1][:, cols],
+                rhs=codes.bitcast(FP8X4),
+                rhs_scale=plane,
+                start=start,
+                stop=stop,
+            )
+
+        h_banks = []
+        for c in range(CHUNKS):
+            cols = slice(CHUNK * c, CHUNK * (c + 1))
+            bank = psum.tile([P, PACK, CHUNK], F32, name="h_bank%d" % c)
+            x_part = x_picked[c // 2][:, CHUNK * (c % 2) : CHUNK * (c % 2 + 1)]
+            for t in range(PACK):
+                mx(bank[:, t, :], w1_q, t, x_part, x_bytes[:, cols], True, False)
+                mx(bank[:, t, :], w2_q, t, e_picked[c][:], e_bytes[:, cols], False, True)
+            h_banks.append(bank)
+
+        w3_dealt = keep.tile([P, PACK, P, PACK], BF16, name="w3_dealt", align_bytes=64)
+        round_and_deal(nc.scalar.copy, w3_dealt, w3_raw[0], 0, 256, 0)
+        round_and_deal(nc.vector.tensor_copy, w3_dealt, w3_raw[1], 0, 256, 64)
+        w3_q = quantize_weight("w3", w3_dealt)
+
+        h_q = []
+        for c in range(CHUNKS):
+            h_bf = keep.tile([P, CHUNK, PACK], BF16, name="h_bf%d" % c, align_bytes=64)
+            nc.scalar.copy(h_bf[:], h_banks[c][:].rearrange("p t n -> p n t"))
+            h_codes = keep.tile([P, CHUNK], U32, name="h_codes%d" % c, align_bytes=64)
+            h_plane = keep.tile([P, CHUNK], U8, name="h_plane%d" % c, align_bytes=64)
+            nc.vector.quantize_mx(
+                out=h_codes[:].bitcast(FP8X4), scales=h_plane[:], in_=h_bf[:].rearrange("p n t -> p (n t)")
+            )
+            h_q.append((h_codes, h_plane))
+
+        y_codes = keep.tile([P, S], U32, name="y_codes", align_bytes=64)
+        y_plane = keep.tile([P, S], U8, name="y_plane", align_bytes=64)
+        y_rows = out_0.rearrange("(p t) n -> p t n", t=PACK)
+        y_words = out_1[0].rearrange("p n t -> p (n t)").bitcast(I32)
+        for c in range(CHUNKS):
+            cols = slice(CHUNK * c, CHUNK * (c + 1))
+            carried = skip_t[c // 2][:, :, CHUNK * (c % 2) : CHUNK * (c % 2 + 1)]
+            bank = psum.tile([P, PACK, CHUNK], F32, name="g_bank%d" % c)
+            for t in range(PACK):
+                mx(bank[:, t, :], w3_q, t, h_q[c][0][:], h_q[c][1][:], True, True)
+            diff = keep.tile([P, PACK, CHUNK], F32, name="diff%d" % c)
+            nc.vector.tensor_tensor(diff[:], h_banks[c][:], carried, ALU.subtract)
+            gate = keep.tile([P, PACK, CHUNK], F32, name="gate%d" % c)
+            nc.scalar.activation(gate[:], bank[:], ACT.Sigmoid)
+            gated = keep.tile([P, PACK, CHUNK], F32, name="gated%d" % c)
+            nc.vector.tensor_tensor(gated[:], gate[:], diff[:], ALU.mult)
+            y = keep.tile([P, PACK, CHUNK], F32, name="y%d" % c)
+            last = c == CHUNKS - 1
+            parts = [slice(0, CHUNK // 2), slice(CHUNK // 2, CHUNK)] if last else [slice(0, CHUNK)]
+            for part in parts:
+                nc.vector.tensor_tensor(y[:, :, part], gated[:, :, part], carried[:, :, part], ALU.add)
+            nc.sync.dma_start(y_rows[:, :, cols], y[:])
+            for part in parts:
+                width = part.stop - part.start
+                at = slice(cols.start + part.start, cols.start + part.stop)
+                y_bf = keep.tile([P, width, PACK], BF16, name="y_bf%d" % at.start, align_bytes=64)
+                nc.scalar.copy(y_bf[:], y[:, :, part].rearrange("p t n -> p n t"))
+                nc.vector.quantize_mx(
+                    out=y_codes[:, at].bitcast(FP8X4), scales=y_plane[:, at], in_=y_bf[:].rearrange("p n t -> p (n t)")
+                )
+            if c == CHUNKS - 2:
+                nc.sync.dma_start(y_words[:, : cols.stop], y_codes[:, : cols.stop].bitcast(I32))
+            if last:
+                nc.sync.dma_start(y_words[:, cols], y_codes[:, cols].bitcast(I32))
+
+        y_scales = out_2[0].bitcast(I32)
+        for q in range(QUADS):
+            queue = nc.sync if q == 0 else nc.scalar
+            queue.dma_start(y_scales[4 * q : 4 * q + 4, :], y_plane[32 * q : 32 * q + 4, :].bitcast(I32))

@@ -38,10 +38,10 @@ def tile_picked_zhwy_lin_po_kernel(
             nc.vector.memset(plane[:].bitcast(I32), 0)
             return plane
 
-        def load_scales(plane, scales):
+        def load_scales(plane, scales, k):
             rows = scales[0].bitcast(I32)
             for q in range(QUADS):
-                nc.sync.dma_start(plane[32 * q : 32 * q + 4, :].bitcast(I32), rows[4 * q : 4 * q + 4, :])
+                nc.sync.dma_start(plane[32 * q + k : 32 * q + k + 4, :].bitcast(I32), rows[4 * q : 4 * q + 4, :])
 
         def load_words(name, words):
             table = keep.tile([P, words.shape[2]], U32, name=name, align_bytes=64)
@@ -49,7 +49,7 @@ def tile_picked_zhwy_lin_po_kernel(
             return table
 
         def load_rows(name, matrix, c0, c1):
-            piece = keep.tile([P, PACK, c1 - c0], F32, name=name)
+            piece = keep.tile([P, PACK, c1 - c0], F32, name=name, tag=name, align_bytes=64)
             nc.sync.dma_start(piece[:], matrix.rearrange("(p j) c -> p j c", j=PACK)[:, :, c0:c1])
             return piece
 
@@ -58,13 +58,20 @@ def tile_picked_zhwy_lin_po_kernel(
         warm = keep.tile([P, 2], F32, name="warm")
         nc.vector.memset(warm[:, 0:1], 0.0)
         nc.scalar.activation(warm[:, 1:2], warm[:, 0:1], ACT.Sigmoid)
-        w1_lo = load_rows("w1_lo", w1, 0, 256)
-        load_scales(x_plane, x_scales)
+        w1_raw = keep.tile([P, PACK, H], F32, name="w1_raw")
+        w2_raw = keep.tile([P, PACK, H], F32, name="w2_raw")
+
+        def load_slots(raw, matrix, j0, j1):
+            nc.sync.dma_start(raw[:, j0:j1, :], matrix.rearrange("(p j) c -> p j c", j=PACK)[:, j0:j1, :])
+
+        load_slots(w1_raw, w1, 0, 2)
+        load_scales(x_plane, x_scales, 0)
         nc.sync.dma_start(offs_t[:], offs)
-        w1_hi = load_rows("w1_hi", w1, 256, 512)
-        w2_raw = [load_rows("w2_raw", w2, 0, 512)]
-        load_scales(e_plane, e_scales)
+        load_slots(w1_raw, w1, 2, 4)
+        load_slots(w2_raw, w2, 0, 3)
+        load_scales(e_plane, e_scales, 4)
         nc.sync.dma_start(tok_t[:], tok)
+        load_slots(w2_raw, w2, 3, 4)
         x_table = load_words("x_table", x_words)
         e_table = load_words("e_table", e_words)
         w3_raw = [load_rows("w3_raw%d" % a, w3, 256 * a, 256 * (a + 1)) for a in range(2)]
@@ -92,13 +99,13 @@ def tile_picked_zhwy_lin_po_kernel(
 
         x_bytes = gather("x_bytes", U8, x_plane, offs_t, 0, S)
         w1_dealt = keep.tile([P, PACK, P, PACK], BF16, name="w1_dealt", align_bytes=64)
-        round_and_deal(nc.scalar.copy, w1_dealt, w1_lo, 0, 256, 0)
-        round_and_deal(nc.vector.tensor_copy, w1_dealt, w1_hi, 0, 256, 64)
+        round_and_deal(nc.scalar.copy, w1_dealt, w1_raw, 0, 176, 0)
+        round_and_deal(nc.vector.tensor_copy, w1_dealt, w1_raw, 176, 512, 44)
         e_bytes = gather("e_bytes", U8, e_plane, tok_t, 0, S)
         w1_q = quantize_weight("w1", w1_dealt)
         w2_dealt = keep.tile([P, PACK, P, PACK], BF16, name="w2_dealt", align_bytes=64)
-        round_and_deal(nc.scalar.copy, w2_dealt, w2_raw[0], 0, 256, 0)
-        round_and_deal(nc.vector.tensor_copy, w2_dealt, w2_raw[0], 256, 512, 64)
+        round_and_deal(nc.scalar.copy, w2_dealt, w2_raw, 0, 256, 0)
+        round_and_deal(nc.vector.tensor_copy, w2_dealt, w2_raw, 256, 512, 64)
         w2_q = quantize_weight("w2", w2_dealt)
         x_picked = [gather("x_picked%d" % a, U32, x_table, offs_t, 256 * a, 256) for a in range(2)]
         e_picked = [gather("e_picked%d" % c, U32, e_table, tok_t, CHUNK * c, CHUNK) for c in range(CHUNKS)]
@@ -115,68 +122,87 @@ def tile_picked_zhwy_lin_po_kernel(
                 stop=stop,
             )
 
-        h_banks = []
-        for c in range(CHUNKS):
-            cols = slice(CHUNK * c, CHUNK * (c + 1))
-            bank = psum.tile([P, PACK, CHUNK], F32, name="h_bank%d" % c)
-            x_part = x_picked[c // 2][:, CHUNK * (c % 2) : CHUNK * (c % 2 + 1)]
-            for t in range(PACK):
-                mx(bank[:, t, :], w1_q, t, x_part, x_bytes[:, cols], True, False)
-                mx(bank[:, t, :], w2_q, t, e_picked[c][:], e_bytes[:, cols], False, True)
-            h_banks.append(bank)
+        h_banks = [psum.tile([P, PACK, CHUNK], F32, name="h_bank%d" % c) for c in range(CHUNKS)]
 
-        w3_dealt = keep.tile([P, PACK, P, PACK], BF16, name="w3_dealt", align_bytes=64)
-        round_and_deal(nc.scalar.copy, w3_dealt, w3_raw[0], 0, 256, 0)
-        round_and_deal(nc.vector.tensor_copy, w3_dealt, w3_raw[1], 0, 256, 64)
+        def x_pass(c, t):
+            x_part = x_picked[c // 2][:, CHUNK * (c % 2) : CHUNK * (c % 2 + 1)]
+            mx(h_banks[c][:, t, :], w1_q, t, x_part, x_bytes[:, CHUNK * c : CHUNK * (c + 1)], True, False)
+
+        def e_pass(c, t):
+            mx(h_banks[c][:, t, :], w2_q, t, e_picked[c][:], e_bytes[4:, CHUNK * c : CHUNK * (c + 1)], False, True)
+
+        for c in range(CHUNKS):
+            x_pass(c, 0)
+        for c in range(CHUNKS):
+            e_pass(c, 0)
+            for t in range(1, PACK):
+                x_pass(c, t)
+                e_pass(c, t)
+
+        w3_dealt = keep.tile([P, PACK, P, PACK], BF16, name="w3_dealt", tag="w3_dealt", align_bytes=64)
+        round_and_deal(nc.vector.tensor_copy, w3_dealt, w3_raw[0], 0, 256, 0)
+        round_and_deal(nc.scalar.copy, w3_dealt, w3_raw[1], 0, 96, 64)
+        round_and_deal(nc.vector.tensor_copy, w3_dealt, w3_raw[1], 96, 256, 88)
         w3_q = quantize_weight("w3", w3_dealt)
 
-        h_q = []
+        h_bf = keep.tile([P, S * PACK], BF16, name="h_bf", tag="w3_raw1", align_bytes=64)
+        h_codes = keep.tile([P, S], U32, name="h_codes", tag="w3_dealt", align_bytes=64)
+        h_plane = keep.tile([P, S], U8, name="h_plane", align_bytes=64)
         for c in range(CHUNKS):
-            h_bf = keep.tile([P, CHUNK, PACK], BF16, name="h_bf%d" % c, align_bytes=64)
-            nc.scalar.copy(h_bf[:], h_banks[c][:].rearrange("p t n -> p n t"))
-            h_codes = keep.tile([P, CHUNK], U32, name="h_codes%d" % c, align_bytes=64)
-            h_plane = keep.tile([P, CHUNK], U8, name="h_plane%d" % c, align_bytes=64)
-            nc.vector.quantize_mx(
-                out=h_codes[:].bitcast(FP8X4), scales=h_plane[:], in_=h_bf[:].rearrange("p n t -> p (n t)")
-            )
-            h_q.append((h_codes, h_plane))
+            cols = slice(CHUNK * c, CHUNK * (c + 1))
+            rounded = h_bf[:, PACK * cols.start : PACK * cols.stop]
+            nc.scalar.copy(rounded.rearrange("p (n t) -> p n t", t=PACK), h_banks[c][:].rearrange("p t n -> p n t"))
+            nc.vector.quantize_mx(out=h_codes[:, cols].bitcast(FP8X4), scales=h_plane[:, cols], in_=rounded)
 
         y_codes = keep.tile([P, S], U32, name="y_codes", align_bytes=64)
         y_plane = keep.tile([P, S], U8, name="y_plane", align_bytes=64)
         y_rows = out_0.rearrange("(p t) n -> p t n", t=PACK)
         y_words = out_1[0].rearrange("p n t -> p (n t)").bitcast(I32)
-        for c in range(CHUNKS):
+
+        def gate_and_diff(c, gate, diff):
             cols = slice(CHUNK * c, CHUNK * (c + 1))
-            carried = skip_t[c // 2][:, :, CHUNK * (c % 2) : CHUNK * (c % 2 + 1)]
             bank = psum.tile([P, PACK, CHUNK], F32, name="g_bank%d" % c)
             for t in range(PACK):
-                mx(bank[:, t, :], w3_q, t, h_q[c][0][:], h_q[c][1][:], True, True)
-            diff = keep.tile([P, PACK, CHUNK], F32, name="diff%d" % c)
-            nc.vector.tensor_tensor(diff[:], h_banks[c][:], carried, ALU.subtract)
-            gate = keep.tile([P, PACK, CHUNK], F32, name="gate%d" % c)
-            nc.scalar.activation(gate[:], bank[:], ACT.Sigmoid)
-            gated = keep.tile([P, PACK, CHUNK], F32, name="gated%d" % c)
+                mx(bank[:, t, :], w3_q, t, h_codes[:, cols], h_plane[:, cols], True, True)
+            carried = skip_t[c // 2][:, :, CHUNK * (c % 2) : CHUNK * (c % 2 + 1)]
+            nc.vector.tensor_tensor(diff, h_banks[c][:], carried, ALU.subtract)
+            nc.scalar.activation(gate, bank[:], ACT.Sigmoid)
+
+        def finish(chunks, parts):
+            first = CHUNK * chunks[0]
+            width = CHUNK * len(chunks)
+            gate = keep.tile([P, PACK, width], F32, name="gate%d" % first)
+            diff = keep.tile([P, PACK, width], F32, name="diff%d" % first)
+            for i, c in enumerate(chunks):
+                at = slice(CHUNK * i, CHUNK * (i + 1))
+                gate_and_diff(c, gate[:, :, at], diff[:, :, at])
+            gated = keep.tile([P, PACK, width], F32, name="gated%d" % first)
             nc.vector.tensor_tensor(gated[:], gate[:], diff[:], ALU.mult)
-            y = keep.tile([P, PACK, CHUNK], F32, name="y%d" % c)
-            last = c == CHUNKS - 1
-            parts = [slice(0, CHUNK // 2), slice(CHUNK // 2, CHUNK)] if last else [slice(0, CHUNK)]
-            for part in parts:
+            carried = skip_t[first // 256][:, :, first % 256 : first % 256 + width]
+            y = keep.tile([P, PACK, width], F32, name="y%d" % first)
+            step = width // parts
+            for a in range(0, width, step):
+                part = slice(a, a + step)
                 nc.vector.tensor_tensor(y[:, :, part], gated[:, :, part], carried[:, :, part], ALU.add)
-            nc.sync.dma_start(y_rows[:, :, cols], y[:])
-            for part in parts:
-                width = part.stop - part.start
-                at = slice(cols.start + part.start, cols.start + part.stop)
-                y_bf = keep.tile([P, width, PACK], BF16, name="y_bf%d" % at.start, align_bytes=64)
-                nc.scalar.copy(y_bf[:], y[:, :, part].rearrange("p t n -> p n t"))
+            nc.sync.dma_start(y_rows[:, :, first : first + width], y[:])
+            for a in range(0, width, step):
+                at = slice(first + a, first + a + step)
+                y_bf = keep.tile([P, step, PACK], BF16, name="y_bf%d" % at.start, align_bytes=64)
+                nc.scalar.copy(y_bf[:], y[:, :, a : a + step].rearrange("p t n -> p n t"))
                 nc.vector.quantize_mx(
                     out=y_codes[:, at].bitcast(FP8X4), scales=y_plane[:, at], in_=y_bf[:].rearrange("p n t -> p (n t)")
                 )
-            if c == CHUNKS - 2:
-                nc.sync.dma_start(y_words[:, : cols.stop], y_codes[:, : cols.stop].bitcast(I32))
-            if last:
-                nc.sync.dma_start(y_words[:, cols], y_codes[:, cols].bitcast(I32))
+
+        def store_words(c0, c1):
+            nc.sync.dma_start(y_words[:, c0:c1], y_codes[:, c0:c1].bitcast(I32))
+
+        finish([0, 1], 1)
+        finish([2], 1)
+        store_words(0, 3 * CHUNK)
+        finish([3], 2)
+        store_words(3 * CHUNK, S)
 
         y_scales = out_2[0].bitcast(I32)
         for q in range(QUADS):
-            queue = nc.sync if q == 0 else nc.scalar
+            queue = nc.sync if q < 2 else nc.scalar
             queue.dma_start(y_scales[4 * q : 4 * q + 4, :], y_plane[32 * q : 32 * q + 4, :].bitcast(I32))

@@ -139,56 +139,52 @@ def tile_picked_zhwy_lin_po_kernel(
                 x_pass(c, t)
                 e_pass(c, t)
 
-        w3_dealt = keep.tile([P, PACK, P, PACK], BF16, name="w3_dealt", tag="w3_dealt", align_bytes=64)
+        w3_dealt = keep.tile([P, PACK, P, PACK], BF16, name="w3_dealt", align_bytes=64)
         round_and_deal(nc.vector.tensor_copy, w3_dealt, w3_raw[0], 0, 256, 0)
         round_and_deal(nc.scalar.copy, w3_dealt, w3_raw[1], 0, 96, 64)
         round_and_deal(nc.vector.tensor_copy, w3_dealt, w3_raw[1], 96, 256, 88)
         w3_q = quantize_weight("w3", w3_dealt)
 
-        h_bf = keep.tile([P, S * PACK], BF16, name="h_bf", tag="w3_raw1", align_bytes=64)
-        h_codes = keep.tile([P, S], U32, name="h_codes", tag="w3_dealt", align_bytes=64)
-        h_plane = keep.tile([P, S], U8, name="h_plane", align_bytes=64)
-        for c in range(CHUNKS):
-            cols = slice(CHUNK * c, CHUNK * (c + 1))
-            rounded = h_bf[:, PACK * cols.start : PACK * cols.stop]
+        h_q = {}
+
+        def quantize_h(c, rounded):
             nc.scalar.copy(rounded.rearrange("p (n t) -> p n t", t=PACK), h_banks[c][:].rearrange("p t n -> p n t"))
-            nc.vector.quantize_mx(out=h_codes[:, cols].bitcast(FP8X4), scales=h_plane[:, cols], in_=rounded)
+            codes = keep.tile([P, CHUNK], U32, name="h_codes%d" % c, tag="h_codes%d" % c, align_bytes=64)
+            plane = keep.tile([P, CHUNK], U8, name="h_plane%d" % c, align_bytes=64)
+            nc.vector.quantize_mx(
+                out=codes[:].bitcast(FP8X4), scales=plane[:], in_=rounded
+            )
+            h_q[c] = (codes, plane)
 
         y_codes = keep.tile([P, S], U32, name="y_codes", align_bytes=64)
         y_plane = keep.tile([P, S], U8, name="y_plane", align_bytes=64)
         y_rows = out_0.rearrange("(p t) n -> p t n", t=PACK)
         y_words = out_1[0].rearrange("p n t -> p (n t)").bitcast(I32)
 
-        def gate_and_diff(c, gate, diff):
+        def finish(c, pool_slots, rounders):
             cols = slice(CHUNK * c, CHUNK * (c + 1))
             bank = psum.tile([P, PACK, CHUNK], F32, name="g_bank%d" % c)
             for t in range(PACK):
-                mx(bank[:, t, :], w3_q, t, h_codes[:, cols], h_plane[:, cols], True, True)
+                mx(bank[:, t, :], w3_q, t, h_q[c][0][:], h_q[c][1][:], True, True)
             carried = skip_t[c // 2][:, :, CHUNK * (c % 2) : CHUNK * (c % 2 + 1)]
-            nc.vector.tensor_tensor(diff, h_banks[c][:], carried, ALU.subtract)
-            nc.scalar.activation(gate, bank[:], ACT.Sigmoid)
-
-        def finish(chunks, parts):
-            first = CHUNK * chunks[0]
-            width = CHUNK * len(chunks)
-            gate = keep.tile([P, PACK, width], F32, name="gate%d" % first)
-            diff = keep.tile([P, PACK, width], F32, name="diff%d" % first)
-            for i, c in enumerate(chunks):
-                at = slice(CHUNK * i, CHUNK * (i + 1))
-                gate_and_diff(c, gate[:, :, at], diff[:, :, at])
-            gated = keep.tile([P, PACK, width], F32, name="gated%d" % first)
-            nc.vector.tensor_tensor(gated[:], gate[:], diff[:], ALU.mult)
-            carried = skip_t[first // 256][:, :, first % 256 : first % 256 + width]
-            y = keep.tile([P, PACK, width], F32, name="y%d" % first)
-            step = width // parts
-            for a in range(0, width, step):
+            diff = keep.tile([P, PACK, CHUNK], F32, name="diff%d" % c)
+            nc.vector.tensor_tensor(diff[:], carried, h_banks[c][:], ALU.subtract)
+            shut = keep.tile([P, PACK, CHUNK], F32, name="shut%d" % c)
+            nc.scalar.activation(shut[:], bank[:], ACT.Sigmoid, scale=-1.0)
+            gated = keep.tile([P, PACK, CHUNK], F32, name="gated%d" % c)
+            nc.gpsimd.tensor_tensor(gated[:, :pool_slots, :], shut[:, :pool_slots, :], diff[:, :pool_slots, :], ALU.mult)
+            if pool_slots < PACK:
+                nc.vector.tensor_tensor(gated[:, pool_slots:, :], shut[:, pool_slots:, :], diff[:, pool_slots:, :], ALU.mult)
+            y = keep.tile([P, PACK, CHUNK], F32, name="y%d" % c)
+            step = CHUNK // len(rounders)
+            for a in range(0, CHUNK, step):
                 part = slice(a, a + step)
-                nc.vector.tensor_tensor(y[:, :, part], gated[:, :, part], carried[:, :, part], ALU.add)
-            nc.sync.dma_start(y_rows[:, :, first : first + width], y[:])
-            for a in range(0, width, step):
-                at = slice(first + a, first + a + step)
+                nc.vector.tensor_tensor(y[:, :, part], h_banks[c][:, :, part], gated[:, :, part], ALU.add)
+            nc.sync.dma_start(y_rows[:, :, cols], y[:])
+            for i, round_copy in enumerate(rounders):
+                at = slice(cols.start + i * step, cols.start + (i + 1) * step)
                 y_bf = keep.tile([P, step, PACK], BF16, name="y_bf%d" % at.start, align_bytes=64)
-                nc.scalar.copy(y_bf[:], y[:, :, a : a + step].rearrange("p t n -> p n t"))
+                round_copy(y_bf[:], y[:, :, i * step : (i + 1) * step].rearrange("p t n -> p n t"))
                 nc.vector.quantize_mx(
                     out=y_codes[:, at].bitcast(FP8X4), scales=y_plane[:, at], in_=y_bf[:].rearrange("p n t -> p (n t)")
                 )
@@ -196,10 +192,16 @@ def tile_picked_zhwy_lin_po_kernel(
         def store_words(c0, c1):
             nc.sync.dma_start(y_words[:, c0:c1], y_codes[:, c0:c1].bitcast(I32))
 
-        finish([0, 1], 1)
-        finish([2], 1)
+        h_bf = keep.tile([P, 3 * CHUNK * PACK], BF16, name="h_bf", tag="w3_raw1", align_bytes=64)
+        for c in range(3):
+            quantize_h(c, h_bf[:, CHUNK * PACK * c : CHUNK * PACK * (c + 1)])
+        finish(0, 4, [nc.scalar.copy])
+        h_last = keep.tile([P, CHUNK * PACK], BF16, name="h_last", tag="h_codes0", align_bytes=64)
+        quantize_h(3, h_last[:])
+        finish(1, 2, [nc.scalar.copy])
+        finish(2, 2, [nc.scalar.copy])
         store_words(0, 3 * CHUNK)
-        finish([3], 2)
+        finish(3, 2, [nc.scalar.copy, nc.vector.tensor_copy])
         store_words(3 * CHUNK, S)
 
         y_scales = out_2[0].bitcast(I32)

@@ -161,7 +161,7 @@ def tile_picked_zhwy_lin_po_kernel(
         y_rows = out_0.rearrange("(p t) n -> p t n", t=PACK)
         y_words = out_1[0].rearrange("p n t -> p (n t)").bitcast(I32)
 
-        def finish(c, pool_slots, rounders):
+        def gate(c, pool_slots):
             cols = slice(CHUNK * c, CHUNK * (c + 1))
             bank = psum.tile([P, PACK, CHUNK], F32, name="g_bank%d" % c)
             for t in range(PACK):
@@ -175,6 +175,10 @@ def tile_picked_zhwy_lin_po_kernel(
             nc.gpsimd.tensor_tensor(gated[:, :pool_slots, :], shut[:, :pool_slots, :], diff[:, :pool_slots, :], ALU.mult)
             if pool_slots < PACK:
                 nc.vector.tensor_tensor(gated[:, pool_slots:, :], shut[:, pool_slots:, :], diff[:, pool_slots:, :], ALU.mult)
+            return gated
+
+        def finish(c, gated, rounders):
+            cols = slice(CHUNK * c, CHUNK * (c + 1))
             y = keep.tile([P, PACK, CHUNK], F32, name="y%d" % c)
             step = CHUNK // len(rounders)
             for a in range(0, CHUNK, step):
@@ -195,13 +199,14 @@ def tile_picked_zhwy_lin_po_kernel(
         h_bf = keep.tile([P, 3 * CHUNK * PACK], BF16, name="h_bf", tag="w3_raw1", align_bytes=64)
         for c in range(3):
             quantize_h(c, h_bf[:, CHUNK * PACK * c : CHUNK * PACK * (c + 1)])
-        finish(0, 4, [nc.scalar.copy])
+        gated = [gate(0, 4)]
         h_last = keep.tile([P, CHUNK * PACK], BF16, name="h_last", tag="h_codes0", align_bytes=64)
         quantize_h(3, h_last[:])
-        finish(1, 2, [nc.scalar.copy])
-        finish(2, 2, [nc.scalar.copy])
+        gated += [gate(1, 3), gate(2, 2), gate(3, 2)]
+        for c in range(CHUNKS - 1):
+            finish(c, gated[c], [nc.scalar.copy])
         store_words(0, 3 * CHUNK)
-        finish(3, 2, [nc.scalar.copy, nc.vector.tensor_copy])
+        finish(3, gated[3], [nc.scalar.copy, nc.vector.tensor_copy])
         store_words(3 * CHUNK, S)
 
         y_scales = out_2[0].bitcast(I32)

from contextlib import ExitStack

import concourse.mybir as mybir

F32 = mybir.dt.float32
BF16 = mybir.dt.bfloat16
I32 = mybir.dt.int32
U32 = mybir.dt.uint32
U16 = mybir.dt.uint16
U8 = mybir.dt.uint8
FP8X4 = mybir.dt.float8_e4m3fn_x4
ALU = mybir.AluOpType
ACT = mybir.ActivationFunctionType

P = 128
PACK = 4
H = 512
S = 512
CHUNK = 128
CHUNKS = S // CHUNK
QUADS = 4
FLOPS = 3 * 2 * 512 * 512 * 512


def tile_picked_zhwy_lin_po_kernel(
    tc, x_words, x_scales, e_words, e_scales, w1, w2, w3, skip, offs, tok, out_0, out_1, out_2
):
    nc = tc.nc
    with ExitStack() as ctx:
        keep = ctx.enter_context(tc.tile_pool(name="keep", bufs=1))
        psum = ctx.enter_context(tc.psum_pool(name="psum", bufs=1))

        offs_t = keep.tile([P, S // 16], U16, name="offs_t")
        tok_t = keep.tile([P, S // 16], U16, name="tok_t")

        def clear_plane(name, scales):
            plane = keep.tile([P, scales.shape[2]], U8, name=name, align_bytes=64)
            nc.vector.memset(plane[:].bitcast(I32), 0)
            return plane

        def load_scales(plane, scales, k):
            rows = scales[0].bitcast(I32)
            for q in range(QUADS):
                nc.sync.dma_start(plane[32 * q + k : 32 * q + k + 4, :].bitcast(I32), rows[4 * q : 4 * q + 4, :])

        def load_words(name, words):
            table = keep.tile([P, words.shape[2]], U32, name=name, align_bytes=64)
            nc.sync.dma_start(table[:].bitcast(I32), words[0].rearrange("p n t -> p (n t)").bitcast(I32))
            return table

        def load_rows(name, matrix, c0, c1):
            piece = keep.tile([P, PACK, c1 - c0], F32, name=name, tag=name, align_bytes=64)
            nc.sync.dma_start(piece[:], matrix.rearrange("(p j) c -> p j c", j=PACK)[:, :, c0:c1])
            return piece

        x_plane = clear_plane("x_plane", x_scales)
        e_plane = clear_plane("e_plane", e_scales)
        warm = keep.tile([P, 2], F32, name="warm")
        nc.vector.memset(warm[:, 0:1], 0.0)
        nc.scalar.activation(warm[:, 1:2], warm[:, 0:1], ACT.Sigmoid)
        w1_raw = keep.tile([P, PACK, H], F32, name="w1_raw")
        w2_raw = keep.tile([P, PACK, H], F32, name="w2_raw")

        def load_slots(raw, matrix, j0, j1):
            nc.sync.dma_start(raw[:, j0:j1, :], matrix.rearrange("(p j) c -> p j c", j=PACK)[:, j0:j1, :])

        load_slots(w1_raw, w1, 0, 2)
        load_scales(x_plane, x_scales, 0)
        nc.sync.dma_start(offs_t[:], offs)
        load_slots(w1_raw, w1, 2, 4)
        load_slots(w2_raw, w2, 0, 3)
        load_scales(e_plane, e_scales, 4)
        nc.sync.dma_start(tok_t[:], tok)
        load_slots(w2_raw, w2, 3, 4)
        x_table = load_words("x_table", x_words)
        e_table = load_words("e_table", e_words)
        w3_raw = [load_rows("w3_raw%d" % a, w3, 256 * a, 256 * (a + 1)) for a in range(2)]
        skip_t = [load_rows("skip_t%d" % a, skip, 256 * a, 256 * (a + 1)) for a in range(2)]

        def round_and_deal(engine_copy, dealt, raw, c0, c1, m0):
            count = (c1 - c0) // PACK
            engine_copy(
                dealt[:, :, m0 : m0 + count, :].rearrange("p t m j -> p m t j"),
                raw[:, :, c0:c1].rearrange("p j (m t) -> p m t j", t=PACK),
            )

        def quantize_weight(name, dealt):
            codes = keep.tile([P, H], U32, name=name + "_codes", align_bytes=64)
            plane = keep.tile([P, H], U8, name=name + "_plane", align_bytes=64)
            nc.vector.quantize_mx(
                out=codes[:].bitcast(FP8X4), scales=plane[:], in_=dealt[:].rearrange("p t m j -> p (t m j)")
            )
            return codes, plane

        def gather(name, dtype, table, offsets, first, count):
            picked = keep.tile([P, count], dtype, name=name, align_bytes=64)
            nc.vector.tensor_copy(picked[:], table[:].indirect(offsets[:, first // 16 : (first + count) // 16]))
            return picked

        x_bytes = gather("x_bytes", U8, x_plane, offs_t, 0, S)
        w1_dealt = keep.tile([P, PACK, P, PACK], BF16, name="w1_dealt", align_bytes=64)
        round_and_deal(nc.scalar.copy, w1_dealt, w1_raw, 0, 176, 0)
        round_and_deal(nc.vector.tensor_copy, w1_dealt, w1_raw, 176, 512, 44)
        e_bytes = gather("e_bytes", U8, e_plane, tok_t, 0, S)
        w1_q = quantize_weight("w1", w1_dealt)
        w2_dealt = keep.tile([P, PACK, P, PACK], BF16, name="w2_dealt", align_bytes=64)
        round_and_deal(nc.scalar.copy, w2_dealt, w2_raw, 0, 256, 0)
        round_and_deal(nc.vector.tensor_copy, w2_dealt, w2_raw, 256, 512, 64)
        w2_q = quantize_weight("w2", w2_dealt)
        x_picked = [gather("x_picked%d" % a, U32, x_table, offs_t, 256 * a, 256) for a in range(2)]
        e_picked = [gather("e_picked%d" % c, U32, e_table, tok_t, CHUNK * c, CHUNK) for c in range(CHUNKS)]

        def mx(out, weight, t, codes, plane, start, stop):
            cols = slice(P * t, P * (t + 1))
            nc.tensor.matmul_mx(
                out=out,
                lhsT=weight[0][:, cols].bitcast(FP8X4),
                lhsT_scale=weight[1][:, cols],
                rhs=codes.bitcast(FP8X4),
                rhs_scale=plane,
                start=start,
                stop=stop,
            )

        h_banks = [psum.tile([P, PACK, CHUNK], F32, name="h_bank%d" % c) for c in range(CHUNKS)]

        def x_pass(c, t):
            x_part = x_picked[c // 2][:, CHUNK * (c % 2) : CHUNK * (c % 2 + 1)]
            mx(h_banks[c][:, t, :], w1_q, t, x_part, x_bytes[:, CHUNK * c : CHUNK * (c + 1)], True, False)

        def e_pass(c, t):
            mx(h_banks[c][:, t, :], w2_q, t, e_picked[c][:], e_bytes[4:, CHUNK * c : CHUNK * (c + 1)], False, True)

        for c in range(CHUNKS):
            x_pass(c, 0)
        for c in range(CHUNKS):
            e_pass(c, 0)
            for t in range(1, PACK):
                x_pass(c, t)
                e_pass(c, t)

        w3_dealt = keep.tile([P, PACK, P, PACK], BF16, name="w3_dealt", align_bytes=64)
        round_and_deal(nc.vector.tensor_copy, w3_dealt, w3_raw[0], 0, 256, 0)
        round_and_deal(nc.scalar.copy, w3_dealt, w3_raw[1], 0, 96, 64)
        round_and_deal(nc.vector.tensor_copy, w3_dealt, w3_raw[1], 96, 256, 88)
        w3_q = quantize_weight("w3", w3_dealt)

        h_q = {}

        def quantize_h(c, rounded):
            nc.scalar.copy(rounded.rearrange("p (n t) -> p n t", t=PACK), h_banks[c][:].rearrange("p t n -> p n t"))
            codes = keep.tile([P, CHUNK], U32, name="h_codes%d" % c, tag="h_codes%d" % c, align_bytes=64)
            plane = keep.tile([P, CHUNK], U8, name="h_plane%d" % c, align_bytes=64)
            nc.vector.quantize_mx(
                out=codes[:].bitcast(FP8X4), scales=plane[:], in_=rounded
            )
            h_q[c] = (codes, plane)

        y_codes = keep.tile([P, S], U32, name="y_codes", align_bytes=64)
        y_plane = keep.tile([P, S], U8, name="y_plane", align_bytes=64)
        y_rows = out_0.rearrange("(p t) n -> p t n", t=PACK)
        y_words = out_1[0].rearrange("p n t -> p (n t)").bitcast(I32)

        def gate(c, pool_slots):
            cols = slice(CHUNK * c, CHUNK * (c + 1))
            bank = psum.tile([P, PACK, CHUNK], F32, name="g_bank%d" % c)
            for t in range(PACK):
                mx(bank[:, t, :], w3_q, t, h_q[c][0][:], h_q[c][1][:], True, True)
            carried = skip_t[c // 2][:, :, CHUNK * (c % 2) : CHUNK * (c % 2 + 1)]
            diff = keep.tile([P, PACK, CHUNK], F32, name="diff%d" % c)
            nc.vector.tensor_tensor(diff[:], carried, h_banks[c][:], ALU.subtract)
            shut = keep.tile([P, PACK, CHUNK], F32, name="shut%d" % c)
            nc.scalar.activation(shut[:], bank[:], ACT.Sigmoid, scale=-1.0)
            gated = keep.tile([P, PACK, CHUNK], F32, name="gated%d" % c)
            nc.gpsimd.tensor_tensor(gated[:, :pool_slots, :], shut[:, :pool_slots, :], diff[:, :pool_slots, :], ALU.mult)
            if pool_slots < PACK:
                nc.vector.tensor_tensor(gated[:, pool_slots:, :], shut[:, pool_slots:, :], diff[:, pool_slots:, :], ALU.mult)
            return gated

        def finish(c, gated, rounders):
            cols = slice(CHUNK * c, CHUNK * (c + 1))
            y = keep.tile([P, PACK, CHUNK], F32, name="y%d" % c)
            step = CHUNK // len(rounders)
            for a in range(0, CHUNK, step):
                part = slice(a, a + step)
                nc.vector.tensor_tensor(y[:, :, part], h_banks[c][:, :, part], gated[:, :, part], ALU.add)
            nc.sync.dma_start(y_rows[:, :, cols], y[:])
            for i, round_copy in enumerate(rounders):
                at = slice(cols.start + i * step, cols.start + (i + 1) * step)
                y_bf = keep.tile([P, step, PACK], BF16, name="y_bf%d" % at.start, align_bytes=64)
                round_copy(y_bf[:], y[:, :, i * step : (i + 1) * step].rearrange("p t n -> p n t"))
                nc.vector.quantize_mx(
                    out=y_codes[:, at].bitcast(FP8X4), scales=y_plane[:, at], in_=y_bf[:].rearrange("p n t -> p (n t)")
                )

        def store_words(c0, c1):
            nc.sync.dma_start(y_words[:, c0:c1], y_codes[:, c0:c1].bitcast(I32))

        h_bf = keep.tile([P, 3 * CHUNK * PACK], BF16, name="h_bf", tag="w3_raw1", align_bytes=64)
        for c in range(3):
            quantize_h(c, h_bf[:, CHUNK * PACK * c : CHUNK * PACK * (c + 1)])
        gated = [gate(0, 4)]
        h_last = keep.tile([P, CHUNK * PACK], BF16, name="h_last", tag="h_codes0", align_bytes=64)
        quantize_h(3, h_last[:])
        gated += [gate(1, 3), gate(2, 2), gate(3, 2)]
        for c in range(CHUNKS - 1):
            finish(c, gated[c], [nc.scalar.copy])
        store_words(0, 3 * CHUNK)
        finish(3, gated[3], [nc.scalar.copy, nc.vector.tensor_copy])
        store_words(3 * CHUNK, S)

        y_scales = out_2[0].bitcast(I32)
        for q in range(QUADS):
            queue = nc.sync if q < 2 else nc.scalar
            queue.dma_start(y_scales[4 * q : 4 * q + 4, :], y_plane[32 * q : 32 * q + 4, :].bitcast(I32))
